import numpy as np, ml_dtypes
CORES = [122,123,126,250,251,254,378,379,382,506,507,510]
N = 12
KB, QP = 1, 256
MEM = [5,7,8]
def setup_inputs(rng):
    q = rng.standard_normal((N, 128, QP), dtype=np.float32) / 4; k = rng.standard_normal((N, 128, KB * 128), dtype=np.float32)
    a = 2 * np.pi * rng.random((N, QP)); s = 400 * rng.random((N, QP)) ** 1.5; q[:, 0, :] = s * np.cos(a); q[:, 1, :] = s * np.sin(a); q[:, 2, :] = 150 * rng.standard_normal((N, QP)); k[:, 2, :] = 1 + k[:, 2, :] / 50
    c = np.zeros(N); c[MEM] = rng.permutation(len(MEM))
    a = (2 * np.pi * rng.random() + np.pi / 2 * (c.reshape(N, 1, 1) + 0.5) / len(MEM) - 0.5 + (np.arange(KB).reshape(1, KB, 1) + rng.random((N, KB, 128))) / KB).reshape(N, KB * 128); k[:, 0, :] = np.cos(a); k[:, 1, :] = np.sin(a)
    return {"q": q.astype(ml_dtypes.bfloat16), "k": k.astype(ml_dtypes.bfloat16), "v": rng.standard_normal((N, 128, KB * 128), dtype=np.float32).astype(ml_dtypes.bfloat16)}
def setup_inputs_big(rng):
    d = setup_inputs(rng)
    for k in ("v",): d[k] = (d[k].astype(np.float32) * 1048576.0).astype(d[k].dtype)
    return d
def setup_inputs_small(rng):
    d = setup_inputs(rng)
    for k in ("v",): d[k] = (d[k].astype(np.float32) * (1 / 1048576.0)).astype(d[k].dtype)
    return d
def reference(q, k, v):
    Q, K, V = q.astype(np.float64), k.astype(np.float64), v.astype(np.float64)
    y = np.zeros((N, QP, 128))
    for r in range(N):
        js = list(MEM)
        S = np.concatenate([K[j].T @ Q[r] for j in js], axis=0)
        P = np.exp(S - S.max(axis=0)); P = P / P.sum(axis=0)
        y[r] = P.T @ np.concatenate([V[j][:, 128 * b:128 * b + 128] for j in js for b in range(KB)], axis=0)
    return {"y": y.astype(ml_dtypes.bfloat16)}

@@ -1,0 +1,279 @@
+from concourse.bass import DstId, RemoteDMATransfer
+from concourse.mybir import AluOpType, AxisListType, ActivationFunctionType
+
+NB = 3
+W = 264
+
+SCRATCH = {
+    "kvd": ("dram", [NB, 128, 256], "bfloat16"),
+    "kv": ("sbuf", [128, NB * W], "bfloat16"),
+    "qs": ("sbuf", [128, 256], "bfloat16"),
+    "ones": ("sbuf", [128, 128], "bfloat16"),
+    "ident": ("sbuf", [128, 128], "bfloat16"),
+    "negm": ("sbuf", [128, 8], "bfloat16"),
+    "dgE": ("sbuf", [128, 256], "bfloat16"),
+    "dgL": ("sbuf", [128, 256], "bfloat16"),
+    "p": ("sbuf", [128, NB * 256], "bfloat16"),
+    "w": ("sbuf", [128, 4], "float32"),
+    "t": ("sbuf", [128, 272], "bfloat16"),
+    "rl": ("sbuf", [128, 4], "float32"),
+    "ys": ("sbuf", [128, 256], "bfloat16"),
+    "stE": ("psum", [128, 512], "float32"),
+    "stL0": ("psum", [128, 512], "float32"),
+    "stL1": ("psum", [128, 512], "float32"),
+    "s0": ("psum", [128, 512], "float32"),
+    "s1": ("psum", [128, 512], "float32"),
+    "s2": ("psum", [128, 512], "float32"),
+    "oE": ("psum", [128, 512], "float32"),
+    "o1": ("psum", [128, 512], "float32"),
+}
+SEMAPHORES = (["ldd", "lds", "ldq", "fill", "idn", "sent", "st", "ste", "ne", "dge", "me", "oe", "dgl", "w", "tt",
+               "stl0", "stl1", "nl0", "nl1", "o0", "o1", "r0", "r1", "y0", "y1"]
+              + ["arr%d" % j for j in range(NB)] + ["cp%d" % j for j in range(NB)]
+              + ["sx%d" % j for j in range(NB)] + ["px%d" % j for j in range(NB)])
+
+
+def _bits(mask):
+    return bin(mask).count("1")
+
+
+def _plan(cores, mem, topo):
+    def place(c):
+        return (topo.host(c), topo.chip(c))
+
+    def lane(src, dsts):
+        m = topo.mask(src, dsts[0])
+        for d in dsts:
+            m &= topo.mask(src, d)
+        return m
+
+    roots = [cores[m] for m in mem]
+    calls = {c: [] for c in cores}
+    arrive = {c: {} for c in cores}
+    jobs = {}
+    for j, root in enumerate(roots):
+        arrive[root][j] = ("own", 0, 0)
+        peers = [c for c in cores if c != root and place(c) == place(root)]
+        away = [c for c in cores if place(c) != place(root)]
+        near = [c for c in away if topo.may_write(root, c)]
+        far = [c for c in away if not topo.may_write(root, c)]
+        relays = []
+        if far:
+            hosts = sorted({topo.host(c) for c in near if all(topo.may_write(c, f) for f in far)},
+                           key=lambda h: (jobs.get(h, 0), sum(topo.host(r) == h for r in roots), h))
+            via = hosts[0]
+            jobs[via] = jobs.get(via, 0) + 1
+            cand = sorted((c for c in near if topo.host(c) == via), key=lambda c: (c in roots, c))
+            r1 = cand[0]
+            rest = sorted(cand[1:], key=lambda c: (c in roots, topo.die(c) == topo.die(r1), c))
+            relays = [r1] + rest[:1]
+        direct = [c for c in near if c not in relays and relays and topo.host(c) == topo.host(relays[0])]
+        direct += [c for c in near if c not in relays and c not in direct]
+        off = lane(root, near) if near else 0
+        for i, c in enumerate(relays):
+            calls[root].append((j, [c], "dram", off))
+            arrive[c][j] = ("dram", 1 + i, _bits(off))
+        if peers:
+            on = (lane(root, peers) & ~off) or lane(root, peers)
+            calls[root].append((j, peers, "sbuf", on))
+            for c in peers:
+                arrive[c][j] = ("sbuf", 0.5, _bits(on))
+        if direct:
+            calls[root].append((j, direct, "sbuf", off))
+            for i, c in enumerate(direct):
+                arrive[c][j] = ("sbuf", 1 + len(relays) + i, _bits(off))
+        if far:
+            r1, r2 = relays[0], relays[-1]
+            fs = sorted(far, key=lambda c: (topo.die(c) != topo.die(r1), c))
+            if r2 != r1:
+                last = sorted(fs, key=lambda c: (topo.die(c) != topo.die(r2), -fs.index(c)))[0]
+                share = [(r1, [c for c in fs if c != last]), (r2, [last])]
+            else:
+                share = [(r1, fs)]
+            for i, (r, ds) in enumerate(share):
+                m = lane(r, ds)
+                calls[r].append((j, ds, "sbuf", m))
+                for n, c in enumerate(ds):
+                    arrive[c][j] = ("sbuf", 6 + i + n, _bits(m))
+    return calls, arrive
+
+
+def rank_program(g, core, T, topo):
+    if T.rank_of(core) is None:
+        return
+    cores, mem = list(T.cores), list(T.tables["MEM"])
+    calls, arrive = _plan(cores, mem, topo)
+    how = arrive[core]
+    S = T.sem
+    tq, vq, aq, sq = g.tensor, g.vector, g.scalar, g.sync
+    mult, amax, X = AluOpType.mult, AluOpType.max, AxisListType.X
+    Exp, Ident = ActivationFunctionType.Exp, ActivationFunctionType.Identity
+    H = (0, 1)
+
+    def kk(j):
+        return T.kv[:, j * W:j * W + 128]
+
+    def v1(j):
+        return T.kv[:, j * W + 128:j * W + 257]
+
+    def blk(j):
+        return T.kv[:, j * W:j * W + 256]
+
+    def qh(h):
+        return T.qs[:, h * 128:(h + 1) * 128]
+
+    def ph(j, h):
+        return T.p[:, j * 256 + h * 128:j * 256 + (h + 1) * 128]
+
+    ready = {}
+    for j in sorted(how):
+        if how[j][0] == "own":
+            sq.dma_start(T.kvd[j, :, 0:128], T.k[:, :]).then_inc(S.ldd, 16)
+            aq.dma_start(T.kvd[j, :, 128:256], T.v[:, :]).then_inc(S.ldd, 16)
+            sq.dma_start(kk(j), T.k[:, :]).then_inc(S.lds, 16)
+            aq.dma_start(T.kv[:, j * W + 128:j * W + 256], T.v[:, :]).then_inc(S.lds, 16)
+            ready[j] = (S.lds, 32)
+    sq.dma_start(T.qs[:, :], T.q[:, :]).then_inc(S.ldq, 16)
+    for j in sorted(how, key=lambda b: how[b][1]):
+        if how[j][0] == "dram":
+            sq.wait_ge(S["arr%d" % j], how[j][2])
+            sq.dma_start(blk(j), T.kvd[j]).then_inc(S["cp%d" % j], 16)
+            ready[j] = (S["cp%d" % j], 16)
+        elif how[j][0] == "sbuf":
+            ready[j] = (S["arr%d" % j], how[j][2])
+
+    vq.memset(T.ones[:, :], 1.0).then_inc(S.fill, 1)
+    for j in range(NB):
+        vq.memset(T.kv[:, j * W + 256:j * W + 264], 1.0).then_inc(S.fill, 1)
+    NF = 1 + NB
+    g.wait_ge(S.fill, NF)
+    g.affine_select(T.ident[:, :], T.ones[:, :], [[-1, 128]], AluOpType.is_equal, 0.0, 0, 1).then_inc(S.idn, 1)
+
+    sent = 0
+    for j, dsts, land, mask in calls[core]:
+        if how[j][0] == "own":
+            g.wait_ge(S.ldd, 32)
+        else:
+            g.wait_ge(S["arr%d" % j], how[j][2])
+        out = T.kvd[j] if land == "dram" else blk(j)
+        at = [topo.addr(d, core) for d in dsts]
+        if len(dsts) == 1:
+            g.remote_dma(out_ap=out, in_ap=T.kvd[j], remote_sem=S["arr%d" % j], local_sem=S.sent,
+                         pid=at[0][1], routing_id=at[0][0], dma_engine_mask=mask)
+        else:
+            ids = [DstId(rid=rid, pnc=pid) for rid, pid in at]
+            g.remote_dma_fused([RemoteDMATransfer(dst_ids=ids, dma_engine_mask=mask, remote_sem=S["arr%d" % j],
+                                                  srcs=[T.kvd[j]], dsts=[out] * len(dsts))], local_sem=S.sent)
+        sent += _bits(mask)
+
+    order = sorted(how, key=lambda b: how[b][1])
+    E = [j for j in order if how[j][1] < 1] or order[:1]
+    L = [j for j in order if j not in E]
+    nE, nL = len(E), len(L)
+    pS = [T.s0, T.s1, T.s2]
+    stL = [T.stL0, T.stL1]
+    O = [pS[E[0]], T.o1]
+
+    tq.wait_ge(S.ldq, 16)
+    tq.wait_ge(S.fill, NF)
+    for e, j in enumerate(E):
+        tq.wait_ge(*ready[j])
+        for h in H:
+            c = (h * nE + e) * 128
+            tq.matmul(T.stE[:, c:c + 128], qh(h), kk(j), True, True).then_inc(S.ste, 1)
+        tq.matmul(pS[j][:, 0:256], kk(j), T.qs[:, :], True, False)
+    tq.wait_ge(S.dge, 2)
+    for j in E:
+        tq.matmul(pS[j][:, 0:256], T.ones[:, :], T.dgE[:, :], False, True).then_inc(S["sx%d" % j], 1)
+
+    def early_sums():
+        for j in E:
+            tq.wait_ge(S["px%d" % j], 1)
+        for h in H:
+            for e, j in enumerate(E):
+                mm = tq.matmul(T.oE[:, h * 256:h * 256 + 129], ph(j, h), v1(j), e == 0, e == nE - 1)
+                if e == nE - 1:
+                    mm.then_inc(S.oe, 1)
+
+    def late_scores():
+        tq.wait_ge(S.me, 2)
+        for l, j in enumerate(L):
+            tq.wait_ge(*ready[j])
+            for h in H:
+                tq.matmul(stL[h][:, l * 128:(l + 1) * 128], qh(h), kk(j), True, True).then_inc(S["stl%d" % h], 1)
+            tq.matmul(pS[j][:, 0:256], kk(j), T.qs[:, :], True, False)
+
+    if nE == 1:
+        late_scores()
+        early_sums()
+    else:
+        early_sums()
+        late_scores()
+    tq.wait_ge(S.dgl, 2)
+    for j in L:
+        tq.matmul(pS[j][:, 0:256], T.ones[:, :], T.dgL[:, :], False, True).then_inc(S["sx%d" % j], 1)
+    tq.wait_ge(S.tt, 2)
+    tq.wait_ge(S.idn, 1)
+    for h in H:
+        tq.matmul(O[h][:, 0:129], T.ident[:, :], T.t[:, h * 136:h * 136 + 129], True, False)
+    for l, j in enumerate(L):
+        tq.wait_ge(S["px%d" % j], 1)
+        for h in H:
+            mm = tq.matmul(O[h][:, 0:129], ph(j, h), v1(j), False, l == nL - 1)
+            if l == nL - 1:
+                mm.then_inc(S["o%d" % h], 1)
+
+    vq.wait_ge(S.ste, 2 * nE)
+    for h in H:
+        vq.tensor_reduce(T.negm[:, h:h + 1], T.stE[:, h * nE * 128:(h + 1) * nE * 128], X, amax,
+                         negate=True).then_inc(S.ne, 1)
+    vq.wait_ge(S.ne, 2)
+    vq.wait_ge(S.idn, 1)
+    for h in H:
+        vq.tensor_scalar(T.dgE[:, h * 128:(h + 1) * 128], T.ident[:, :], T.negm[:, h:h + 1], None,
+                         mult).then_inc(S.dge, 1)
+    for h in H:
+        vq.tensor_scalar(stL[h][:, nL * 128:nL * 128 + 1], T.negm[:, h:h + 1], -1.0, None, mult).then_inc(S.me, 1)
+    for h in H:
+        vq.wait_ge(S["stl%d" % h], nL)
+        if h == 0:
+            vq.wait_ge(S.me, 2)
+        vq.tensor_reduce(T.negm[:, 2 + h:3 + h], stL[h][:, 0:nL * 128 + 1], X, amax,
+                         negate=True).then_inc(S["nl%d" % h], 1)
+    for h in H:
+        vq.wait_ge(S["nl%d" % h], 1)
+        vq.tensor_scalar(T.dgL[:, h * 128:(h + 1) * 128], T.ident[:, :], T.negm[:, 2 + h:3 + h], None,
+                         mult).then_inc(S.dgl, 1)
+    vq.wait_ge(S.w, 2)
+    vq.wait_ge(S.oe, 2)
+    for h in H:
+        vq.tensor_scalar(T.t[:, h * 136:h * 136 + 129], T.oE[:, h * 256:h * 256 + 129], T.w[:, h:h + 1], None,
+                         mult).then_inc(S.tt, 1)
+    for h in H:
+        vq.wait_ge(S["o%d" % h], 1)
+        vq.reciprocal(T.rl[:, h:h + 1], O[h][:, 128:129]).then_inc(S["r%d" % h], 1)
+    vq.wait_ge(S.r0, 1)
+    vq.tensor_scalar(T.ys[:, 0:128], O[0][:, 0:128], T.rl[:, 0:1], None, mult).then_inc(S.y0, 1)
+
+    for j in E:
+        aq.wait_ge(S["sx%d" % j], 1)
+        aq.activation(T.p[:, j * 256:(j + 1) * 256], pS[j][:, 0:256], Exp).then_inc(S["px%d" % j], 1)
+    aq.wait_ge(S.ne, 2)
+    for h in H:
+        aq.wait_ge(S["nl%d" % h], 1)
+        aq.activation(T.w[:, h:h + 1], T.negm[:, h:h + 1], Exp, bias=T.negm[:, 2 + h:3 + h],
+                      scale=-1.0).then_inc(S.w, 1)
+    for j in L:
+        aq.wait_ge(S["sx%d" % j], 1)
+        aq.activation(T.p[:, j * 256:(j + 1) * 256], pS[j][:, 0:256], Exp).then_inc(S["px%d" % j], 1)
+    aq.wait_ge(S.r1, 1)
+    aq.activation(T.ys[:, 128:256], T.o1[:, 0:128], Ident, scale=T.rl[:, 1:2]).then_inc(S.y1, 1)
+    aq.wait_ge(S.y1, 1)
+    aq.dma_start(T.y[128:256, :], T.ys[:, 128:256]).then_inc(S.st, 16)
+
+    sq.wait_ge(S.y0, 1)
+    sq.dma_start(T.y[0:128, :], T.ys[:, 0:128]).then_inc(S.st, 16)
+
+    if sent:
+        g.wait_ge(S.sent, sent)
+    g.wait_ge(S.st, 32)

@@ -2,7 +2,7 @@ from concourse.bass import DstId, RemoteDMATransfer
 from concourse.mybir import AluOpType, AxisListType, ActivationFunctionType
 
 NB = 3
-W = 264
+W = 256
 
 SCRATCH = {
     "kvd": ("dram", [NB, 128, 256], "bfloat16"),
@@ -10,31 +10,46 @@ SCRATCH = {
     "qs": ("sbuf", [128, 256], "bfloat16"),
     "ones": ("sbuf", [128, 128], "bfloat16"),
     "ident": ("sbuf", [128, 128], "bfloat16"),
-    "negm": ("sbuf", [128, 8], "bfloat16"),
-    "dgE": ("sbuf", [128, 256], "bfloat16"),
-    "dgL": ("sbuf", [128, 256], "bfloat16"),
-    "p": ("sbuf", [128, NB * 256], "bfloat16"),
+    "nm": ("sbuf", [128, 4], "float32"),
+    "pE": ("sbuf", [128, 512], "bfloat16"),
+    "pL": ("sbuf", [128, 512], "bfloat16"),
+    "ptE": ("sbuf", [128, 512], "bfloat16"),
+    "ptL": ("sbuf", [128, 512], "bfloat16"),
+    "lE": ("sbuf", [128, 4], "float32"),
+    "lL": ("sbuf", [128, 4], "float32"),
+    "ls": ("sbuf", [128, 4], "float32"),
     "w": ("sbuf", [128, 4], "float32"),
-    "t": ("sbuf", [128, 272], "bfloat16"),
+    "la": ("sbuf", [128, 4], "float32"),
     "rl": ("sbuf", [128, 4], "float32"),
+    "tE": ("sbuf", [128, 256], "float32"),
+    "u": ("sbuf", [128, 256], "float32"),
     "ys": ("sbuf", [128, 256], "bfloat16"),
     "stE": ("psum", [128, 512], "float32"),
     "stL0": ("psum", [128, 512], "float32"),
     "stL1": ("psum", [128, 512], "float32"),
-    "s0": ("psum", [128, 512], "float32"),
-    "s1": ("psum", [128, 512], "float32"),
-    "s2": ("psum", [128, 512], "float32"),
+    "trE": ("psum", [128, 1024], "bfloat16"),
+    "trL0": ("psum", [128, 1024], "bfloat16"),
+    "trL1": ("psum", [128, 1024], "bfloat16"),
     "oE": ("psum", [128, 512], "float32"),
-    "o1": ("psum", [128, 512], "float32"),
 }
-SEMAPHORES = (["ldd", "lds", "ldq", "fill", "idn", "sent", "st", "ste", "ne", "dge", "me", "oe", "dgl", "w", "tt",
-               "stl0", "stl1", "nl0", "nl1", "o0", "o1", "r0", "r1", "y0", "y1"]
-              + ["arr%d" % j for j in range(NB)] + ["cp%d" % j for j in range(NB)]
-              + ["sx%d" % j for j in range(NB)] + ["px%d" % j for j in range(NB)])
+SEMAPHORES = (["ldd", "lds", "ldq", "fill", "idn", "sent", "st", "ste", "ne", "me", "pxe", "tre", "cpe", "oe",
+               "stl0", "stl1", "nl0", "nl1", "px00", "px01", "px10", "px11", "ls0", "ls1", "trl0", "trl1",
+               "cpl0", "cpl1", "w", "las", "rs", "te", "o0", "o1", "u0", "u1", "y0", "y1"]
+              + ["arr%d" % j for j in range(NB)] + ["cp%d" % j for j in range(NB)])
 
 
 def _bits(mask):
     return bin(mask).count("1")
+
+
+def _alternate(mask):
+    out, take = 0, True
+    for b in range(mask.bit_length()):
+        if mask >> b & 1:
+            if take:
+                out |= 1 << b
+            take = not take
+    return out
 
 
 def _plan(cores, mem, topo):
@@ -57,44 +72,41 @@ def _plan(cores, mem, topo):
         away = [c for c in cores if place(c) != place(root)]
         near = [c for c in away if topo.may_write(root, c)]
         far = [c for c in away if not topo.may_write(root, c)]
-        relays = []
-        if far:
-            hosts = sorted({topo.host(c) for c in near if all(topo.may_write(c, f) for f in far)},
-                           key=lambda h: (jobs.get(h, 0), sum(topo.host(r) == h for r in roots), h))
-            via = hosts[0]
-            jobs[via] = jobs.get(via, 0) + 1
-            cand = sorted((c for c in near if topo.host(c) == via), key=lambda c: (c in roots, c))
-            r1 = cand[0]
-            rest = sorted(cand[1:], key=lambda c: (c in roots, topo.die(c) == topo.die(r1), c))
-            relays = [r1] + rest[:1]
-        direct = [c for c in near if c not in relays and relays and topo.host(c) == topo.host(relays[0])]
-        direct += [c for c in near if c not in relays and c not in direct]
-        off = lane(root, near) if near else 0
+        hosts = sorted({topo.host(c) for c in near if all(topo.may_write(c, f) for f in far)},
+                       key=lambda h: (jobs.get(h, 0), sum(topo.host(r) == h for r in roots), h))
+        via = hosts[0]
+        jobs[via] = jobs.get(via, 0) + 1
+        cand = sorted((c for c in near if topo.host(c) == via), key=lambda c: (c in roots, c))
+        r1 = cand[0]
+        rest = sorted(cand[1:], key=lambda c: (c in roots, topo.die(c) == topo.die(r1), c))
+        relays = [r1] + rest[:1]
+        third = [c for c in near if c not in relays and topo.host(c) == via]
+        others = [c for c in near if topo.host(c) != via]
+        off = lane(root, near)
+        la = _alternate(off)
+        lb = off & ~la
+        calls[root].append([(j, relays[:1], "dram", la), (j, others, "sbuf", lb)])
+        calls[root].append([(j, relays[1:], "dram", la)])
         for i, c in enumerate(relays):
-            calls[root].append((j, [c], "dram", off))
-            arrive[c][j] = ("dram", 1 + i, _bits(off))
+            arrive[c][j] = ("dram", 4 + i, _bits(la))
+        for i, c in enumerate(others):
+            arrive[c][j] = ("sbuf", 1.5 + i, _bits(lb))
         if peers:
             on = (lane(root, peers) & ~off) or lane(root, peers)
-            calls[root].append((j, peers, "sbuf", on))
+            calls[root].append([(j, peers, "sbuf", on)])
             for c in peers:
                 arrive[c][j] = ("sbuf", 0.5, _bits(on))
-        if direct:
-            calls[root].append((j, direct, "sbuf", off))
-            for i, c in enumerate(direct):
-                arrive[c][j] = ("sbuf", 1 + len(relays) + i, _bits(off))
-        if far:
-            r1, r2 = relays[0], relays[-1]
-            fs = sorted(far, key=lambda c: (topo.die(c) != topo.die(r1), c))
-            if r2 != r1:
-                last = sorted(fs, key=lambda c: (topo.die(c) != topo.die(r2), -fs.index(c)))[0]
-                share = [(r1, [c for c in fs if c != last]), (r2, [last])]
-            else:
-                share = [(r1, fs)]
-            for i, (r, ds) in enumerate(share):
-                m = lane(r, ds)
-                calls[r].append((j, ds, "sbuf", m))
-                for n, c in enumerate(ds):
-                    arrive[c][j] = ("sbuf", 6 + i + n, _bits(m))
+        calls[root].append([(j, third, "sbuf", la)])
+        for i, c in enumerate(third):
+            arrive[c][j] = ("sbuf", 3 + i, _bits(la))
+        r2 = relays[-1]
+        fs = sorted(far, key=lambda c: (topo.die(c) != topo.die(r1), c))
+        last = sorted(fs, key=lambda c: (topo.die(c) != topo.die(r2), -fs.index(c)))[0]
+        for i, (r, ds) in enumerate([(r1, [c for c in fs if c != last]), (r2, [last])]):
+            m = lane(r, ds)
+            calls[r].append([(j, ds, "sbuf", m)])
+            for n, c in enumerate(ds):
+                arrive[c][j] = ("sbuf", 6 + i + n, _bits(m))
     return calls, arrive
 
 
@@ -106,24 +118,24 @@ def rank_program(g, core, T, topo):
     how = arrive[core]
     S = T.sem
     tq, vq, aq, sq = g.tensor, g.vector, g.scalar, g.sync
-    mult, amax, X = AluOpType.mult, AluOpType.max, AxisListType.X
+    mult, add, amax, X = AluOpType.mult, AluOpType.add, AluOpType.max, AxisListType.X
     Exp, Ident = ActivationFunctionType.Exp, ActivationFunctionType.Identity
     H = (0, 1)
 
     def kk(j):
         return T.kv[:, j * W:j * W + 128]
 
-    def v1(j):
-        return T.kv[:, j * W + 128:j * W + 257]
+    def vv(j):
+        return T.kv[:, j * W + 128:j * W + 256]
 
     def blk(j):
         return T.kv[:, j * W:j * W + 256]
 
-    def qh(h):
-        return T.qs[:, h * 128:(h + 1) * 128]
+    def half(t, h):
+        return t[:, h * 128:(h + 1) * 128]
 
-    def ph(j, h):
-        return T.p[:, j * 256 + h * 128:j * 256 + (h + 1) * 128]
+    def col(t, c):
+        return t[:, c:c + 1]
 
     ready = {}
     for j in sorted(how):
@@ -131,7 +143,7 @@ def rank_program(g, core, T, topo):
             sq.dma_start(T.kvd[j, :, 0:128], T.k[:, :]).then_inc(S.ldd, 16)
             aq.dma_start(T.kvd[j, :, 128:256], T.v[:, :]).then_inc(S.ldd, 16)
             sq.dma_start(kk(j), T.k[:, :]).then_inc(S.lds, 16)
-            aq.dma_start(T.kv[:, j * W + 128:j * W + 256], T.v[:, :]).then_inc(S.lds, 16)
+            aq.dma_start(vv(j), T.v[:, :]).then_inc(S.lds, 16)
             ready[j] = (S.lds, 32)
     sq.dma_start(T.qs[:, :], T.q[:, :]).then_inc(S.ldq, 16)
     for j in sorted(how, key=lambda b: how[b][1]):
@@ -143,136 +155,127 @@ def rank_program(g, core, T, topo):
             ready[j] = (S["arr%d" % j], how[j][2])
 
     vq.memset(T.ones[:, :], 1.0).then_inc(S.fill, 1)
-    for j in range(NB):
-        vq.memset(T.kv[:, j * W + 256:j * W + 264], 1.0).then_inc(S.fill, 1)
-    NF = 1 + NB
-    g.wait_ge(S.fill, NF)
+    g.wait_ge(S.fill, 1)
     g.affine_select(T.ident[:, :], T.ones[:, :], [[-1, 128]], AluOpType.is_equal, 0.0, 0, 1).then_inc(S.idn, 1)
 
     sent = 0
-    for j, dsts, land, mask in calls[core]:
-        if how[j][0] == "own":
-            g.wait_ge(S.ldd, 32)
-        else:
-            g.wait_ge(S["arr%d" % j], how[j][2])
-        out = T.kvd[j] if land == "dram" else blk(j)
-        at = [topo.addr(d, core) for d in dsts]
-        if len(dsts) == 1:
-            g.remote_dma(out_ap=out, in_ap=T.kvd[j], remote_sem=S["arr%d" % j], local_sem=S.sent,
-                         pid=at[0][1], routing_id=at[0][0], dma_engine_mask=mask)
-        else:
-            ids = [DstId(rid=rid, pnc=pid) for rid, pid in at]
-            g.remote_dma_fused([RemoteDMATransfer(dst_ids=ids, dma_engine_mask=mask, remote_sem=S["arr%d" % j],
-                                                  srcs=[T.kvd[j]], dsts=[out] * len(dsts))], local_sem=S.sent)
-        sent += _bits(mask)
+    for call in calls[core]:
+        trs = []
+        for j, dsts, land, mask in call:
+            if how[j][0] == "own":
+                g.wait_ge(S.ldd, 32)
+            else:
+                g.wait_ge(S["arr%d" % j], how[j][2])
+            out = T.kvd[j] if land == "dram" else blk(j)
+            ids = [DstId(rid=a[0], pnc=a[1]) for a in (topo.addr(d, core) for d in dsts)]
+            trs.append(RemoteDMATransfer(dst_ids=ids, dma_engine_mask=mask, remote_sem=S["arr%d" % j],
+                                         srcs=[T.kvd[j]], dsts=[out] * len(dsts)))
+            sent += _bits(mask)
+        g.remote_dma_fused(trs, local_sem=S.sent)
 
     order = sorted(how, key=lambda b: how[b][1])
     E = [j for j in order if how[j][1] < 1] or order[:1]
     L = [j for j in order if j not in E]
     nE, nL = len(E), len(L)
-    pS = [T.s0, T.s1, T.s2]
     stL = [T.stL0, T.stL1]
-    O = [pS[E[0]], T.o1]
+    trL = [T.trL0, T.trL1]
+    O = [T.stE[:, 0:128], T.stL0[:, 0:128]]
 
     tq.wait_ge(S.ldq, 16)
-    tq.wait_ge(S.fill, NF)
+    tq.wait_ge(S.idn, 1)
     for e, j in enumerate(E):
         tq.wait_ge(*ready[j])
         for h in H:
-            c = (h * nE + e) * 128
-            tq.matmul(T.stE[:, c:c + 128], qh(h), kk(j), True, True).then_inc(S.ste, 1)
-        tq.matmul(pS[j][:, 0:256], kk(j), T.qs[:, :], True, False)
-    tq.wait_ge(S.dge, 2)
-    for j in E:
-        tq.matmul(pS[j][:, 0:256], T.ones[:, :], T.dgE[:, :], False, True).then_inc(S["sx%d" % j], 1)
-
-    def early_sums():
-        for j in E:
-            tq.wait_ge(S["px%d" % j], 1)
-        for h in H:
-            for e, j in enumerate(E):
-                mm = tq.matmul(T.oE[:, h * 256:h * 256 + 129], ph(j, h), v1(j), e == 0, e == nE - 1)
-                if e == nE - 1:
-                    mm.then_inc(S.oe, 1)
-
-    def late_scores():
-        tq.wait_ge(S.me, 2)
-        for l, j in enumerate(L):
-            tq.wait_ge(*ready[j])
-            for h in H:
-                tq.matmul(stL[h][:, l * 128:(l + 1) * 128], qh(h), kk(j), True, True).then_inc(S["stl%d" % h], 1)
-            tq.matmul(pS[j][:, 0:256], kk(j), T.qs[:, :], True, False)
-
-    if nE == 1:
-        late_scores()
-        early_sums()
-    else:
-        early_sums()
-        late_scores()
-    tq.wait_ge(S.dgl, 2)
-    for j in L:
-        tq.matmul(pS[j][:, 0:256], T.ones[:, :], T.dgL[:, :], False, True).then_inc(S["sx%d" % j], 1)
-    tq.wait_ge(S.tt, 2)
-    tq.wait_ge(S.idn, 1)
+            c = h * 256 + e * 128
+            tq.matmul(T.stE[:, c:c + 128], half(T.qs, h), kk(j), True, True).then_inc(S.ste, 1)
+    tq.wait_ge(S.pxe, 2)
     for h in H:
-        tq.matmul(O[h][:, 0:129], T.ident[:, :], T.t[:, h * 136:h * 136 + 129], True, False)
-    for l, j in enumerate(L):
-        tq.wait_ge(S["px%d" % j], 1)
-        for h in H:
-            mm = tq.matmul(O[h][:, 0:129], ph(j, h), v1(j), False, l == nL - 1)
+        for e in range(nE):
+            c = (h * nE + e) * 128
+            tq.transpose(T.trE[:, c:c + 128], T.pE[:, h * 256 + e * 128:h * 256 + (e + 1) * 128],
+                         T.ident[:, :]).then_inc(S.tre, 1)
+    tq.wait_ge(S.cpe, 1)
+    for h in H:
+        for e, j in enumerate(E):
+            c = (h * nE + e) * 128
+            mm = tq.matmul(half(T.oE, h), T.ptE[:, c:c + 128], vv(j), e == 0, e == nE - 1)
+            if e == nE - 1:
+                mm.then_inc(S.oe, 1)
+    tq.wait_ge(S.me, 2)
+    if all(how[j][1] >= 6 for j in L):
+        turns = [(l, h) for h in H for l in range(nL)]
+    else:
+        turns = [(l, h) for l in range(nL) for h in H]
+    for l, h in turns:
+        tq.wait_ge(*ready[L[l]])
+        tq.matmul(stL[h][:, l * 128:(l + 1) * 128], half(T.qs, h), kk(L[l]), True, True).then_inc(S["stl%d" % h], 1)
+    for h in H:
+        for l in range(nL):
+            tq.wait_ge(S["px%d%d" % (h, l)], 1)
+            tq.transpose(trL[h][:, l * 128:(l + 1) * 128], T.pL[:, h * 256 + l * 128:h * 256 + (l + 1) * 128],
+                         T.ident[:, :]).then_inc(S["trl%d" % h], 1)
+    tq.wait_ge(S.ne, 2)
+    tq.wait_ge(S.nl0, 1)
+    for h in H:
+        tq.wait_ge(S["cpl%d" % h], 1)
+        for l, j in enumerate(L):
+            mm = tq.matmul(O[h], T.ptL[:, h * 256 + l * 128:h * 256 + (l + 1) * 128], vv(j), l == 0, l == nL - 1)
             if l == nL - 1:
                 mm.then_inc(S["o%d" % h], 1)
 
     vq.wait_ge(S.ste, 2 * nE)
     for h in H:
-        vq.tensor_reduce(T.negm[:, h:h + 1], T.stE[:, h * nE * 128:(h + 1) * nE * 128], X, amax,
-                         negate=True).then_inc(S.ne, 1)
+        vq.tensor_reduce(col(T.nm, h), T.stE[:, h * 256:h * 256 + nE * 128], X, amax, negate=True).then_inc(S.ne, 1)
     vq.wait_ge(S.ne, 2)
-    vq.wait_ge(S.idn, 1)
     for h in H:
-        vq.tensor_scalar(T.dgE[:, h * 128:(h + 1) * 128], T.ident[:, :], T.negm[:, h:h + 1], None,
-                         mult).then_inc(S.dge, 1)
-    for h in H:
-        vq.tensor_scalar(stL[h][:, nL * 128:nL * 128 + 1], T.negm[:, h:h + 1], -1.0, None, mult).then_inc(S.me, 1)
+        vq.tensor_scalar(col(stL[h], nL * 128), col(T.nm, h), -1.0, None, mult).then_inc(S.me, 1)
+    vq.wait_ge(S.tre, 2 * nE)
+    vq.tensor_copy(T.ptE[:, 0:2 * nE * 128], T.trE[:, 0:2 * nE * 128]).then_inc(S.cpe, 1)
+    vq.wait_ge(S.me, 2)
     for h in H:
         vq.wait_ge(S["stl%d" % h], nL)
-        if h == 0:
-            vq.wait_ge(S.me, 2)
-        vq.tensor_reduce(T.negm[:, 2 + h:3 + h], stL[h][:, 0:nL * 128 + 1], X, amax,
-                         negate=True).then_inc(S["nl%d" % h], 1)
+        vq.tensor_reduce(col(T.nm, 2 + h), stL[h][:, 0:nL * 128 + 1], X, amax, negate=True).then_inc(S["nl%d" % h], 1)
     for h in H:
-        vq.wait_ge(S["nl%d" % h], 1)
-        vq.tensor_scalar(T.dgL[:, h * 128:(h + 1) * 128], T.ident[:, :], T.negm[:, 2 + h:3 + h], None,
-                         mult).then_inc(S.dgl, 1)
-    vq.wait_ge(S.w, 2)
-    vq.wait_ge(S.oe, 2)
-    for h in H:
-        vq.tensor_scalar(T.t[:, h * 136:h * 136 + 129], T.oE[:, h * 256:h * 256 + 129], T.w[:, h:h + 1], None,
-                         mult).then_inc(S.tt, 1)
+        for l in range(nL):
+            vq.wait_ge(S["px%d%d" % (h, l)], 1)
+        vq.tensor_reduce(col(T.ls, h), T.lL[:, 2 * h:2 * h + nL], X, add).then_inc(S["ls%d" % h], 1)
+        vq.wait_ge(S["trl%d" % h], nL)
+        vq.tensor_copy(T.ptL[:, h * 256:h * 256 + nL * 128], trL[h][:, 0:nL * 128]).then_inc(S["cpl%d" % h], 1)
+    vq.wait_ge(S.las, 2)
+    vq.reciprocal(T.rl[:, 0:2], T.la[:, 0:2]).then_inc(S.rs, 1)
+    vq.wait_ge(S.te, 2)
     for h in H:
         vq.wait_ge(S["o%d" % h], 1)
-        vq.reciprocal(T.rl[:, h:h + 1], O[h][:, 128:129]).then_inc(S["r%d" % h], 1)
-    vq.wait_ge(S.r0, 1)
-    vq.tensor_scalar(T.ys[:, 0:128], O[0][:, 0:128], T.rl[:, 0:1], None, mult).then_inc(S.y0, 1)
+        vq.tensor_tensor(half(T.u, h), O[h], half(T.tE, h), add).then_inc(S["u%d" % h], 1)
 
-    for j in E:
-        aq.wait_ge(S["sx%d" % j], 1)
-        aq.activation(T.p[:, j * 256:(j + 1) * 256], pS[j][:, 0:256], Exp).then_inc(S["px%d" % j], 1)
     aq.wait_ge(S.ne, 2)
     for h in H:
+        aq.activation(T.pE[:, h * 256:h * 256 + nE * 128], T.stE[:, h * 256:h * 256 + nE * 128], Exp,
+                      bias=col(T.nm, h), accum_out=col(T.lE, h)).then_inc(S.pxe, 1)
+    for h in H:
         aq.wait_ge(S["nl%d" % h], 1)
-        aq.activation(T.w[:, h:h + 1], T.negm[:, h:h + 1], Exp, bias=T.negm[:, 2 + h:3 + h],
-                      scale=-1.0).then_inc(S.w, 1)
-    for j in L:
-        aq.wait_ge(S["sx%d" % j], 1)
-        aq.activation(T.p[:, j * 256:(j + 1) * 256], pS[j][:, 0:256], Exp).then_inc(S["px%d" % j], 1)
-    aq.wait_ge(S.r1, 1)
-    aq.activation(T.ys[:, 128:256], T.o1[:, 0:128], Ident, scale=T.rl[:, 1:2]).then_inc(S.y1, 1)
+        for l in range(nL):
+            aq.activation(T.pL[:, h * 256 + l * 128:h * 256 + (l + 1) * 128], stL[h][:, l * 128:(l + 1) * 128], Exp,
+                          bias=col(T.nm, 2 + h), accum_out=col(T.lL, 2 * h + l)).then_inc(S["px%d%d" % (h, l)], 1)
+    for h in H:
+        aq.activation(col(T.w, h), col(T.nm, h), Exp, bias=col(T.nm, 2 + h), scale=-1.0).then_inc(S.w, 1)
+    aq.wait_ge(S.w, 2)
+    aq.wait_ge(S.pxe, 2)
+    for h in H:
+        aq.wait_ge(S["ls%d" % h], 1)
+        aq.activation(col(T.la, h), col(T.lE, h), Ident, bias=col(T.ls, h), scale=col(T.w, h)).then_inc(S.las, 1)
+    aq.wait_ge(S.oe, 2)
+    for h in H:
+        aq.activation(half(T.tE, h), half(T.oE, h), Ident, scale=col(T.w, h)).then_inc(S.te, 1)
+    aq.wait_ge(S.rs, 1)
+    for h in H:
+        aq.wait_ge(S["u%d" % h], 1)
+        aq.activation(half(T.ys, h), half(T.u, h), Ident, scale=col(T.rl, h)).then_inc(S["y%d" % h], 1)
     aq.wait_ge(S.y1, 1)
-    aq.dma_start(T.y[128:256, :], T.ys[:, 128:256]).then_inc(S.st, 16)
+    aq.dma_start(T.y[128:256, :], half(T.ys, 1)).then_inc(S.st, 16)
 
     sq.wait_ge(S.y0, 1)
-    sq.dma_start(T.y[0:128, :], T.ys[:, 0:128]).then_inc(S.st, 16)
+    sq.dma_start(T.y[0:128, :], half(T.ys, 0)).then_inc(S.st, 16)
 
     if sent:
         g.wait_ge(S.sent, sent)

@@ -3,9 +3,11 @@ from concourse.mybir import AluOpType, AxisListType, ActivationFunctionType
 
 NB = 3
 W = 256
+WORLD = 512
 
 SCRATCH = {
-    "kvd": ("dram", [NB, 128, 256], "bfloat16"),
+    "kd": ("dram", [NB, 128, 128], "bfloat16"),
+    "vd": ("dram", [NB, 128, 128], "bfloat16"),
     "kv": ("sbuf", [128, NB * W], "bfloat16"),
     "qs": ("sbuf", [128, 256], "bfloat16"),
     "ones": ("sbuf", [128, 128], "bfloat16"),
@@ -32,10 +34,11 @@ SCRATCH = {
     "trL1": ("psum", [128, 1024], "bfloat16"),
     "oE": ("psum", [128, 512], "float32"),
 }
-SEMAPHORES = (["ldd", "lds", "ldq", "fill", "idn", "sent", "st", "ste", "ne", "me", "pxe", "tre", "cpe", "oe",
+SEMAPHORES = (["ldk", "ldv", "lds", "ldq", "fill", "idn", "sent", "st", "ste", "ne", "me", "pxe", "tre", "cpe", "oe",
                "stl0", "stl1", "nl0", "nl1", "px00", "px01", "px10", "px11", "ls0", "ls1", "trl0", "trl1",
                "cpl0", "cpl1", "w", "las", "rs", "te", "o0", "o1", "u0", "u1", "y0", "y1"]
-              + ["arr%d" % j for j in range(NB)] + ["cp%d" % j for j in range(NB)])
+              + ["arr%s%d" % (p, j) for p in ("k", "v", "kv") for j in range(NB)]
+              + ["cp%s%d" % (p, j) for p in ("k", "v") for j in range(NB)])
 
 
 def _bits(mask):
@@ -63,10 +66,12 @@ def _plan(cores, mem, topo):
         return m
 
     roots = [cores[m] for m in mem]
-    calls = {c: [] for c in cores}
+    calls = {}
     arrive = {c: {} for c in cores}
     jobs = {}
+    busy = []
     for j, root in enumerate(roots):
+        mine = calls.setdefault(root, [])
         arrive[root][j] = ("own", 0, 0)
         peers = [c for c in cores if c != root and place(c) == place(root)]
         away = [c for c in cores if place(c) != place(root)]
@@ -76,46 +81,73 @@ def _plan(cores, mem, topo):
                        key=lambda h: (jobs.get(h, 0), sum(topo.host(r) == h for r in roots), h))
         via = hosts[0]
         jobs[via] = jobs.get(via, 0) + 1
-        cand = sorted((c for c in near if topo.host(c) == via), key=lambda c: (c in roots, c))
-        r1 = cand[0]
-        rest = sorted(cand[1:], key=lambda c: (c in roots, topo.die(c) == topo.die(r1), c))
-        relays = [r1] + rest[:1]
-        third = [c for c in near if c not in relays and topo.host(c) == via]
-        others = [c for c in near if topo.host(c) != via]
+
+        def free(h):
+            return sorted(c for c in near if topo.host(c) == h and c not in roots and c not in busy)
+
+        fa = free(via)
+        fa = fa[:1] + sorted(fa[1:], key=lambda c: (topo.die(c) == topo.die(fa[0]), c))
+        ra = fa[:2]
+        rb = [c for h in hosts[1:] for c in free(h)][:1]
+        need = len(far) - len(ra) - len(rb)
+        if need > 0:
+            spot = [c for c in near if topo.host(c) == via][0]
+            idle = sorted((c for c in range(WORLD) if place(c) == place(spot) and c not in cores and c not in busy
+                           and topo.may_write(root, c) and all(topo.may_write(c, f) for f in far)),
+                          key=lambda c: (sum(place(r) == place(c) and topo.die(r) == topo.die(c) for r in roots), c))
+            ra = ra + idle[:need]
+        busy.extend(ra + rb)
         off = lane(root, near)
         la = _alternate(off)
         lb = off & ~la
-        calls[root].append([(j, relays[:1], "dram", la), (j, others, "sbuf", lb)])
-        calls[root].append([(j, relays[1:], "dram", la)])
-        for i, c in enumerate(relays):
-            arrive[c][j] = ("dram", 4 + i, _bits(la))
-        for i, c in enumerate(others):
-            arrive[c][j] = ("sbuf", 1.5 + i, _bits(lb))
+        qa = [("k", c) for c in ra] + [("v", c) for c in ra]
+        qb = [("k", c) for c in rb] + [("v", c) for c in rb]
+        for i in range(max(len(qa), len(qb))):
+            call = []
+            if i < len(qa):
+                call.append((j, qa[i][0], [qa[i][1]], "dram", la))
+            if i < len(qb):
+                call.append((j, qb[i][0], [qb[i][1]], "dram", lb))
+            mine.append(call)
+        for c in ra:
+            arrive.setdefault(c, {})[j] = ("dram", 2, _bits(la))
+        for c in rb:
+            arrive.setdefault(c, {})[j] = ("dram", 2, _bits(lb))
         if peers:
             on = (lane(root, peers) & ~off) or lane(root, peers)
-            calls[root].append([(j, peers, "sbuf", on)])
+            mine.append([(j, "kv", peers, "sbuf", on)])
             for c in peers:
-                arrive[c][j] = ("sbuf", 0.5, _bits(on))
-        calls[root].append([(j, third, "sbuf", la)])
-        for i, c in enumerate(third):
-            arrive[c][j] = ("sbuf", 3 + i, _bits(la))
-        r2 = relays[-1]
-        fs = sorted(far, key=lambda c: (topo.die(c) != topo.die(r1), c))
-        last = sorted(fs, key=lambda c: (topo.die(c) != topo.die(r2), -fs.index(c)))[0]
-        for i, (r, ds) in enumerate([(r1, [c for c in fs if c != last]), (r2, [last])]):
-            m = lane(r, ds)
-            calls[r].append([(j, ds, "sbuf", m)])
-            for n, c in enumerate(ds):
-                arrive[c][j] = ("sbuf", 6 + i + n, _bits(m))
+                arrive[c][j] = ("whole", 0.5, _bits(on))
+        mates = {r: [] for r in ra + rb}
+        for rs, ds in ((ra, [c for c in near if topo.host(c) == via and c not in ra]),
+                       (rb, [c for c in near if topo.host(c) != via and c not in rb])):
+            for i, c in enumerate(ds):
+                mates[rs[i % len(rs)]].append(c)
+        left = list(far)
+        for r in ra + rb:
+            d = sorted(left, key=lambda c: (topo.die(c) != topo.die(r), c))[0]
+            left.remove(d)
+            m = lane(r, [d])
+            arrive[d][j] = ("parts", 6, _bits(m))
+            on = 0
+            if mates[r]:
+                on = (lane(r, mates[r]) & ~m) or lane(r, mates[r])
+                for c in mates[r]:
+                    arrive[c][j] = ("parts", 4, _bits(on))
+            for part in ("k", "v"):
+                call = [(j, part, [d], "sbuf", m)]
+                if mates[r]:
+                    call.append((j, part, mates[r], "sbuf", on))
+                calls.setdefault(r, []).append(call)
     return calls, arrive
 
 
 def rank_program(g, core, T, topo):
-    if T.rank_of(core) is None:
-        return
     cores, mem = list(T.cores), list(T.tables["MEM"])
     calls, arrive = _plan(cores, mem, topo)
-    how = arrive[core]
+    how = arrive.get(core)
+    if not how:
+        return
     S = T.sem
     tq, vq, aq, sq = g.tensor, g.vector, g.scalar, g.sync
     mult, add, amax, X = AluOpType.mult, AluOpType.add, AluOpType.max, AxisListType.X
@@ -137,41 +169,62 @@ def rank_program(g, core, T, topo):
     def col(t, c):
         return t[:, c:c + 1]
 
-    ready = {}
+    def send_all():
+        sent = 0
+        for call in calls.get(core, []):
+            trs = []
+            for j, part, dsts, land, mask in call:
+                if how[j][0] == "own":
+                    g.wait_ge(*{"k": (S.ldk, 16), "v": (S.ldv, 16), "kv": (S.lds, 32)}[part])
+                else:
+                    g.wait_ge(S["arr%s%d" % (part, j)], how[j][2])
+                piece = {"k": T.kd[j], "v": T.vd[j], "kv": blk(j)}[part]
+                out = piece if land == "dram" else {"k": kk(j), "v": vv(j), "kv": blk(j)}[part]
+                ids = [DstId(rid=a[0], pnc=a[1]) for a in (topo.addr(d, core) for d in dsts)]
+                trs.append(RemoteDMATransfer(dst_ids=ids, dma_engine_mask=mask, remote_sem=S["arr%s%d" % (part, j)],
+                                             srcs=[piece], dsts=[out] * len(dsts)))
+                sent += _bits(mask)
+            g.remote_dma_fused(trs, local_sem=S.sent)
+        return sent
+
+    if T.rank_of(core) is None:
+        g.wait_ge(S.sent, send_all())
+        return
+
+    rk, rv = {}, {}
+    is_root = False
     for j in sorted(how):
         if how[j][0] == "own":
-            sq.dma_start(T.kvd[j, :, 0:128], T.k[:, :]).then_inc(S.ldd, 16)
-            aq.dma_start(T.kvd[j, :, 128:256], T.v[:, :]).then_inc(S.ldd, 16)
+            is_root = True
+            sq.dma_start(T.kd[j], T.k[:, :]).then_inc(S.ldk, 16)
+            aq.dma_start(T.vd[j], T.v[:, :]).then_inc(S.ldv, 16)
             sq.dma_start(kk(j), T.k[:, :]).then_inc(S.lds, 16)
             aq.dma_start(vv(j), T.v[:, :]).then_inc(S.lds, 16)
-            ready[j] = (S.lds, 32)
+            rk[j] = rv[j] = (S.lds, 32)
     sq.dma_start(T.qs[:, :], T.q[:, :]).then_inc(S.ldq, 16)
     for j in sorted(how, key=lambda b: how[b][1]):
         if how[j][0] == "dram":
-            sq.wait_ge(S["arr%d" % j], how[j][2])
-            sq.dma_start(blk(j), T.kvd[j]).then_inc(S["cp%d" % j], 16)
-            ready[j] = (S["cp%d" % j], 16)
-        elif how[j][0] == "sbuf":
-            ready[j] = (S["arr%d" % j], how[j][2])
+            sq.wait_ge(S["arrk%d" % j], how[j][2])
+            sq.dma_start(kk(j), T.kd[j]).then_inc(S["cpk%d" % j], 16)
+            sq.wait_ge(S["arrv%d" % j], how[j][2])
+            sq.dma_start(vv(j), T.vd[j]).then_inc(S["cpv%d" % j], 16)
+            rk[j], rv[j] = (S["cpk%d" % j], 16), (S["cpv%d" % j], 16)
+        elif how[j][0] == "whole":
+            rk[j] = rv[j] = (S["arrkv%d" % j], how[j][2])
+        elif how[j][0] == "parts":
+            rk[j], rv[j] = (S["arrk%d" % j], how[j][2]), (S["arrv%d" % j], how[j][2])
 
     vq.memset(T.ones[:, :], 1.0).then_inc(S.fill, 1)
-    g.wait_ge(S.fill, 1)
-    g.affine_select(T.ident[:, :], T.ones[:, :], [[-1, 128]], AluOpType.is_equal, 0.0, 0, 1).then_inc(S.idn, 1)
 
-    sent = 0
-    for call in calls[core]:
-        trs = []
-        for j, dsts, land, mask in call:
-            if how[j][0] == "own":
-                g.wait_ge(S.ldd, 32)
-            else:
-                g.wait_ge(S["arr%d" % j], how[j][2])
-            out = T.kvd[j] if land == "dram" else blk(j)
-            ids = [DstId(rid=a[0], pnc=a[1]) for a in (topo.addr(d, core) for d in dsts)]
-            trs.append(RemoteDMATransfer(dst_ids=ids, dma_engine_mask=mask, remote_sem=S["arr%d" % j],
-                                         srcs=[T.kvd[j]], dsts=[out] * len(dsts)))
-            sent += _bits(mask)
-        g.remote_dma_fused(trs, local_sem=S.sent)
+    def identity():
+        g.wait_ge(S.fill, 1)
+        g.affine_select(T.ident[:, :], T.ones[:, :], [[-1, 128]], AluOpType.is_equal, 0.0, 0, 1).then_inc(S.idn, 1)
+
+    if not is_root:
+        identity()
+    sent = send_all()
+    if is_root:
+        identity()
 
     order = sorted(how, key=lambda b: how[b][1])
     E = [j for j in order if how[j][1] < 1] or order[:1]
@@ -184,7 +237,7 @@ def rank_program(g, core, T, topo):
     tq.wait_ge(S.ldq, 16)
     tq.wait_ge(S.idn, 1)
     for e, j in enumerate(E):
-        tq.wait_ge(*ready[j])
+        tq.wait_ge(*rk[j])
         for h in H:
             c = h * 256 + e * 128
             tq.matmul(T.stE[:, c:c + 128], half(T.qs, h), kk(j), True, True).then_inc(S.ste, 1)
@@ -195,6 +248,8 @@ def rank_program(g, core, T, topo):
             tq.transpose(T.trE[:, c:c + 128], T.pE[:, h * 256 + e * 128:h * 256 + (e + 1) * 128],
                          T.ident[:, :]).then_inc(S.tre, 1)
     tq.wait_ge(S.cpe, 1)
+    for j in E:
+        tq.wait_ge(*rv[j])
     for h in H:
         for e, j in enumerate(E):
             c = (h * nE + e) * 128
@@ -207,7 +262,7 @@ def rank_program(g, core, T, topo):
     else:
         turns = [(l, h) for l in range(nL) for h in H]
     for l, h in turns:
-        tq.wait_ge(*ready[L[l]])
+        tq.wait_ge(*rk[L[l]])
         tq.matmul(stL[h][:, l * 128:(l + 1) * 128], half(T.qs, h), kk(L[l]), True, True).then_inc(S["stl%d" % h], 1)
     for h in H:
         for l in range(nL):
@@ -216,6 +271,8 @@ def rank_program(g, core, T, topo):
                          T.ident[:, :]).then_inc(S["trl%d" % h], 1)
     tq.wait_ge(S.ne, 2)
     tq.wait_ge(S.nl0, 1)
+    for j in L:
+        tq.wait_ge(*rv[j])
     for h in H:
         tq.wait_ge(S["cpl%d" % h], 1)
         for l, j in enumerate(L):

@@ -4,13 +4,15 @@ from concourse.mybir import AluOpType, AxisListType, ActivationFunctionType
 NB = 3
 W = 256
 WORLD = 512
+_MEMO = {}
 
 SCRATCH = {
     "kd": ("dram", [NB, 128, 128], "bfloat16"),
     "vd": ("dram", [NB, 128, 128], "bfloat16"),
     "kv": ("sbuf", [128, NB * W], "bfloat16"),
     "qs": ("sbuf", [128, 256], "bfloat16"),
-    "ones": ("sbuf", [128, 128], "bfloat16"),
+    "zer": ("sbuf", [128, 128], "bfloat16"),
+    "sel": ("sbuf", [128, 128], "bfloat16"),
     "ident": ("sbuf", [128, 128], "bfloat16"),
     "nm": ("sbuf", [128, 4], "float32"),
     "pE": ("sbuf", [128, 512], "bfloat16"),
@@ -34,8 +36,8 @@ SCRATCH = {
     "trL1": ("psum", [128, 1024], "bfloat16"),
     "oE": ("psum", [128, 512], "float32"),
 }
-SEMAPHORES = (["ldk", "ldv", "lds", "ldq", "fill", "idn", "sent", "st", "ste", "ne", "me", "pxe", "tre", "cpe", "oe",
-               "stl0", "stl1", "nl0", "nl1", "px00", "px01", "px10", "px11", "ls0", "ls1", "trl0", "trl1",
+SEMAPHORES = (["ldk", "ldv", "lds", "ldq", "fill", "msk", "idn", "sent", "st", "ste", "ne", "me", "pxe", "tre", "cpe",
+               "oe", "stl0", "stl1", "nl0", "nl1", "px00", "px01", "px10", "px11", "ls0", "ls1", "trl0", "trl1",
                "cpl0", "cpl1", "w", "las", "rs", "te", "o0", "o1", "u0", "u1", "y0", "y1"]
               + ["arr%s%d" % (p, j) for p in ("k", "v", "kv") for j in range(NB)]
               + ["cp%s%d" % (p, j) for p in ("k", "v") for j in range(NB)])
@@ -65,10 +67,17 @@ def _plan(cores, mem, topo):
             m &= topo.mask(src, d)
         return m
 
+    groups = {}
+
+    def group(c):
+        if c not in groups:
+            x = [d for d in range(WORLD) if topo.mates(c, d)][0]
+            groups[c] = (place(c), topo.die(c), topo.may_write(c, x))
+        return groups[c]
+
     roots = [cores[m] for m in mem]
     calls = {}
     arrive = {c: {} for c in cores}
-    jobs = {}
     busy = []
     for j, root in enumerate(roots):
         mine = calls.setdefault(root, [])
@@ -78,24 +87,27 @@ def _plan(cores, mem, topo):
         near = [c for c in away if topo.may_write(root, c)]
         far = [c for c in away if not topo.may_write(root, c)]
         hosts = sorted({topo.host(c) for c in near if all(topo.may_write(c, f) for f in far)},
-                       key=lambda h: (jobs.get(h, 0), sum(topo.host(r) == h for r in roots), h))
+                       key=lambda h: (topo.rack(h) != topo.rack(topo.host(root)), h))
         via = hosts[0]
-        jobs[via] = jobs.get(via, 0) + 1
 
-        def free(h):
-            return sorted(c for c in near if topo.host(c) == h and c not in roots and c not in busy)
+        def pick(h, n, taken):
+            spot = [c for c in near if topo.host(c) == h][0]
+            pool = [c for c in range(WORLD) if place(c) == place(spot) and c not in roots
+                    and topo.may_write(root, c) and all(topo.may_write(c, f) for f in far)]
+            cabled = topo.rack(h) != topo.rack(topo.host(far[0]))
+            out = []
+            for _ in range(n):
+                used = busy + taken + out
+                cand = [c for c in pool if c not in used]
+                if cabled:
+                    cand = [c for c in cand if group(c) not in [group(r) for r in used]] or cand
+                cand.sort(key=lambda c: (c not in cores,
+                                         sum(place(r) == place(c) and topo.die(r) == topo.die(c) for r in used), c))
+                out.append(cand[0])
+            return out
 
-        fa = free(via)
-        fa = fa[:1] + sorted(fa[1:], key=lambda c: (topo.die(c) == topo.die(fa[0]), c))
-        ra = fa[:2]
-        rb = [c for h in hosts[1:] for c in free(h)][:1]
-        need = len(far) - len(ra) - len(rb)
-        if need > 0:
-            spot = [c for c in near if topo.host(c) == via][0]
-            idle = sorted((c for c in range(WORLD) if place(c) == place(spot) and c not in cores and c not in busy
-                           and topo.may_write(root, c) and all(topo.may_write(c, f) for f in far)),
-                          key=lambda c: (sum(place(r) == place(c) and topo.die(r) == topo.die(c) for r in roots), c))
-            ra = ra + idle[:need]
+        ra = pick(via, len(far) - 1, [])
+        rb = pick(hosts[1], 1, ra)
         busy.extend(ra + rb)
         off = lane(root, near)
         la = _alternate(off)
@@ -144,7 +156,9 @@ def _plan(cores, mem, topo):
 
 def rank_program(g, core, T, topo):
     cores, mem = list(T.cores), list(T.tables["MEM"])
-    calls, arrive = _plan(cores, mem, topo)
+    if "plan" not in _MEMO:
+        _MEMO["plan"] = _plan(cores, mem, topo)
+    calls, arrive = _MEMO["plan"]
     how = arrive.get(core)
     if not how:
         return
@@ -214,48 +228,55 @@ def rank_program(g, core, T, topo):
         elif how[j][0] == "parts":
             rk[j], rv[j] = (S["arrk%d" % j], how[j][2]), (S["arrv%d" % j], how[j][2])
 
-    vq.memset(T.ones[:, :], 1.0).then_inc(S.fill, 1)
+    vq.memset(T.zer[:, :], 0.0).then_inc(S.fill, 1)
 
-    def identity():
+    def mask_diag():
         g.wait_ge(S.fill, 1)
-        g.affine_select(T.ident[:, :], T.ones[:, :], [[-1, 128]], AluOpType.is_equal, 0.0, 0, 1).then_inc(S.idn, 1)
+        g.affine_select(T.sel[:, :], T.zer[:, :], [[-1, 128]], AluOpType.is_equal, -200.0, 0, 1).then_inc(S.msk, 1)
 
     if not is_root:
-        identity()
+        mask_diag()
     sent = send_all()
     if is_root:
-        identity()
+        mask_diag()
+    aq.wait_ge(S.msk, 1)
+    aq.activation(T.ident[:, :], T.sel[:, :], Exp).then_inc(S.idn, 1)
 
     order = sorted(how, key=lambda b: how[b][1])
     E = [j for j in order if how[j][1] < 1] or order[:1]
     L = [j for j in order if j not in E]
     nE, nL = len(E), len(L)
+    tardy = how[E[0]][1] >= 4
     stL = [T.stL0, T.stL1]
     trL = [T.trL0, T.trL1]
     O = [T.stE[:, 0:128], T.stL0[:, 0:128]]
 
+    def early_pv():
+        tq.wait_ge(S.cpe, 1)
+        for j in E:
+            tq.wait_ge(*rv[j])
+        for h in H:
+            for e, j in enumerate(E):
+                c = (h * nE + e) * 128
+                mm = tq.matmul(half(T.oE, h), T.ptE[:, c:c + 128], vv(j), e == 0, e == nE - 1)
+                if e == nE - 1:
+                    mm.then_inc(S.oe, 1)
+
     tq.wait_ge(S.ldq, 16)
-    tq.wait_ge(S.idn, 1)
     for e, j in enumerate(E):
         tq.wait_ge(*rk[j])
         for h in H:
             c = h * 256 + e * 128
             tq.matmul(T.stE[:, c:c + 128], half(T.qs, h), kk(j), True, True).then_inc(S.ste, 1)
+    tq.wait_ge(S.idn, 1)
     tq.wait_ge(S.pxe, 2)
     for h in H:
         for e in range(nE):
             c = (h * nE + e) * 128
             tq.transpose(T.trE[:, c:c + 128], T.pE[:, h * 256 + e * 128:h * 256 + (e + 1) * 128],
                          T.ident[:, :]).then_inc(S.tre, 1)
-    tq.wait_ge(S.cpe, 1)
-    for j in E:
-        tq.wait_ge(*rv[j])
-    for h in H:
-        for e, j in enumerate(E):
-            c = (h * nE + e) * 128
-            mm = tq.matmul(half(T.oE, h), T.ptE[:, c:c + 128], vv(j), e == 0, e == nE - 1)
-            if e == nE - 1:
-                mm.then_inc(S.oe, 1)
+    if not tardy:
+        early_pv()
     tq.wait_ge(S.me, 2)
     if all(how[j][1] >= 6 for j in L):
         turns = [(l, h) for h in H for l in range(nL)]
@@ -264,6 +285,8 @@ def rank_program(g, core, T, topo):
     for l, h in turns:
         tq.wait_ge(*rk[L[l]])
         tq.matmul(stL[h][:, l * 128:(l + 1) * 128], half(T.qs, h), kk(L[l]), True, True).then_inc(S["stl%d" % h], 1)
+    if tardy:
+        early_pv()
     for h in H:
         for l in range(nL):
             tq.wait_ge(S["px%d%d" % (h, l)], 1)

from concourse.bass import DstId, RemoteDMATransfer
from concourse.mybir import AluOpType, AxisListType, ActivationFunctionType

NB = 3
W = 256
WORLD = 512
_MEMO = {}

SCRATCH = {
    "kd": ("dram", [NB, 128, 128], "bfloat16"),
    "vd": ("dram", [NB, 128, 128], "bfloat16"),
    "kv": ("sbuf", [128, NB * W], "bfloat16"),
    "qs": ("sbuf", [128, 256], "bfloat16"),
    "zer": ("sbuf", [128, 128], "bfloat16"),
    "sel": ("sbuf", [128, 128], "bfloat16"),
    "ident": ("sbuf", [128, 128], "bfloat16"),
    "nm": ("sbuf", [128, 4], "float32"),
    "pE": ("sbuf", [128, 512], "bfloat16"),
    "pL": ("sbuf", [128, 512], "bfloat16"),
    "ptE": ("sbuf", [128, 512], "bfloat16"),
    "ptL": ("sbuf", [128, 512], "bfloat16"),
    "lE": ("sbuf", [128, 4], "float32"),
    "lL": ("sbuf", [128, 4], "float32"),
    "ls": ("sbuf", [128, 4], "float32"),
    "w": ("sbuf", [128, 4], "float32"),
    "la": ("sbuf", [128, 4], "float32"),
    "rl": ("sbuf", [128, 4], "float32"),
    "tE": ("sbuf", [128, 256], "float32"),
    "u": ("sbuf", [128, 256], "float32"),
    "ys": ("sbuf", [128, 256], "bfloat16"),
    "stE": ("psum", [128, 512], "float32"),
    "stL0": ("psum", [128, 512], "float32"),
    "stL1": ("psum", [128, 512], "float32"),
    "trE": ("psum", [128, 1024], "bfloat16"),
    "trL0": ("psum", [128, 1024], "bfloat16"),
    "trL1": ("psum", [128, 1024], "bfloat16"),
    "oE": ("psum", [128, 512], "float32"),
}
SEMAPHORES = (["ldk", "ldv", "lds", "ldq", "fill", "msk", "idn", "sent", "st", "ste", "ne", "me", "pxe", "tre", "cpe",
               "oe", "stl0", "stl1", "nl0", "nl1", "px00", "px01", "px10", "px11", "ls0", "ls1", "trl0", "trl1",
               "cpl0", "cpl1", "w", "las", "rs", "te", "o0", "o1", "u0", "u1", "y0", "y1"]
              + ["arr%s%d" % (p, j) for p in ("k", "v", "kv") for j in range(NB)]
              + ["cp%s%d" % (p, j) for p in ("k", "v") for j in range(NB)])


def _bits(mask):
    return bin(mask).count("1")


def _alternate(mask):
    out, take = 0, True
    for b in range(mask.bit_length()):
        if mask >> b & 1:
            if take:
                out |= 1 << b
            take = not take
    return out


def _plan(cores, mem, topo):
    def place(c):
        return (topo.host(c), topo.chip(c))

    def lane(src, dsts):
        m = topo.mask(src, dsts[0])
        for d in dsts:
            m &= topo.mask(src, d)
        return m

    groups = {}

    def group(c):
        if c not in groups:
            x = [d for d in range(WORLD) if topo.mates(c, d)][0]
            groups[c] = (place(c), topo.die(c), topo.may_write(c, x))
        return groups[c]

    roots = [cores[m] for m in mem]
    calls = {}
    arrive = {c: {} for c in cores}
    busy = []
    for j, root in enumerate(roots):
        mine = calls.setdefault(root, [])
        arrive[root][j] = ("own", 0, 0)
        peers = [c for c in cores if c != root and place(c) == place(root)]
        away = [c for c in cores if place(c) != place(root)]
        near = [c for c in away if topo.may_write(root, c)]
        far = [c for c in away if not topo.may_write(root, c)]
        hosts = sorted({topo.host(c) for c in near if all(topo.may_write(c, f) for f in far)},
                       key=lambda h: (topo.rack(h) != topo.rack(topo.host(root)), h))
        via = hosts[0]

        def pick(h, n, taken):
            spot = [c for c in near if topo.host(c) == h][0]
            pool = [c for c in range(WORLD) if place(c) == place(spot) and c not in roots
                    and topo.may_write(root, c) and all(topo.may_write(c, f) for f in far)]
            cabled = topo.rack(h) != topo.rack(topo.host(far[0]))
            out = []
            for _ in range(n):
                used = busy + taken + out
                cand = [c for c in pool if c not in used]
                if cabled:
                    cand = [c for c in cand if group(c) not in [group(r) for r in used]] or cand
                cand.sort(key=lambda c: (c not in cores,
                                         sum(place(r) == place(c) and topo.die(r) == topo.die(c) for r in used), c))
                out.append(cand[0])
            return out

        ra = pick(via, len(far) - 1, [])
        rb = pick(hosts[1], 1, ra)
        busy.extend(ra + rb)
        off = lane(root, near)
        la = _alternate(off)
        lb = off & ~la
        qa = [("k", c) for c in ra] + [("v", c) for c in ra]
        qb = [("k", c) for c in rb] + [("v", c) for c in rb]
        for i in range(max(len(qa), len(qb))):
            call = []
            if i < len(qa):
                call.append((j, qa[i][0], [qa[i][1]], "dram", la))
            if i < len(qb):
                call.append((j, qb[i][0], [qb[i][1]], "dram", lb))
            mine.append(call)
        for c in ra:
            arrive.setdefault(c, {})[j] = ("dram", 2, _bits(la))
        for c in rb:
            arrive.setdefault(c, {})[j] = ("dram", 2, _bits(lb))
        if peers:
            on = (lane(root, peers) & ~off) or lane(root, peers)
            mine.append([(j, "kv", peers, "sbuf", on)])
            for c in peers:
                arrive[c][j] = ("whole", 0.5, _bits(on))
        mates = {r: [] for r in ra + rb}
        for rs, ds in ((ra, [c for c in near if topo.host(c) == via and c not in ra]),
                       (rb, [c for c in near if topo.host(c) != via and c not in rb])):
            for i, c in enumerate(ds):
                mates[rs[i % len(rs)]].append(c)
        left = list(far)
        for r in ra + rb:
            d = sorted(left, key=lambda c: (topo.die(c) != topo.die(r), c))[0]
            left.remove(d)
            m = lane(r, [d])
            arrive[d][j] = ("parts", 6, _bits(m))
            on = 0
            if mates[r]:
                on = (lane(r, mates[r]) & ~m) or lane(r, mates[r])
                for c in mates[r]:
                    arrive[c][j] = ("parts", 4, _bits(on))
            for part in ("k", "v"):
                call = [(j, part, [d], "sbuf", m)]
                if mates[r]:
                    call.append((j, part, mates[r], "sbuf", on))
                calls.setdefault(r, []).append(call)
    return calls, arrive


def rank_program(g, core, T, topo):
    cores, mem = list(T.cores), list(T.tables["MEM"])
    if "plan" not in _MEMO:
        _MEMO["plan"] = _plan(cores, mem, topo)
    calls, arrive = _MEMO["plan"]
    how = arrive.get(core)
    if not how:
        return
    S = T.sem
    tq, vq, aq, sq = g.tensor, g.vector, g.scalar, g.sync
    mult, add, amax, X = AluOpType.mult, AluOpType.add, AluOpType.max, AxisListType.X
    Exp, Ident = ActivationFunctionType.Exp, ActivationFunctionType.Identity
    H = (0, 1)

    def kk(j):
        return T.kv[:, j * W:j * W + 128]

    def vv(j):
        return T.kv[:, j * W + 128:j * W + 256]

    def blk(j):
        return T.kv[:, j * W:j * W + 256]

    def half(t, h):
        return t[:, h * 128:(h + 1) * 128]

    def col(t, c):
        return t[:, c:c + 1]

    def send_all():
        sent = 0
        for call in calls.get(core, []):
            trs = []
            for j, part, dsts, land, mask in call:
                if how[j][0] == "own":
                    g.wait_ge(*{"k": (S.ldk, 16), "v": (S.ldv, 16), "kv": (S.lds, 32)}[part])
                else:
                    g.wait_ge(S["arr%s%d" % (part, j)], how[j][2])
                piece = {"k": T.kd[j], "v": T.vd[j], "kv": blk(j)}[part]
                out = piece if land == "dram" else {"k": kk(j), "v": vv(j), "kv": blk(j)}[part]
                ids = [DstId(rid=a[0], pnc=a[1]) for a in (topo.addr(d, core) for d in dsts)]
                trs.append(RemoteDMATransfer(dst_ids=ids, dma_engine_mask=mask, remote_sem=S["arr%s%d" % (part, j)],
                                             srcs=[piece], dsts=[out] * len(dsts)))
                sent += _bits(mask)
            g.remote_dma_fused(trs, local_sem=S.sent)
        return sent

    if T.rank_of(core) is None:
        g.wait_ge(S.sent, send_all())
        return

    rk, rv = {}, {}
    is_root = False
    for j in sorted(how):
        if how[j][0] == "own":
            is_root = True
            sq.dma_start(T.kd[j], T.k[:, :]).then_inc(S.ldk, 16)
            aq.dma_start(T.vd[j], T.v[:, :]).then_inc(S.ldv, 16)
            sq.dma_start(kk(j), T.k[:, :]).then_inc(S.lds, 16)
            aq.dma_start(vv(j), T.v[:, :]).then_inc(S.lds, 16)
            rk[j] = rv[j] = (S.lds, 32)
    sq.dma_start(T.qs[:, :], T.q[:, :]).then_inc(S.ldq, 16)
    for j in sorted(how, key=lambda b: how[b][1]):
        if how[j][0] == "dram":
            sq.wait_ge(S["arrk%d" % j], how[j][2])
            sq.dma_start(kk(j), T.kd[j]).then_inc(S["cpk%d" % j], 16)
            sq.wait_ge(S["arrv%d" % j], how[j][2])
            sq.dma_start(vv(j), T.vd[j]).then_inc(S["cpv%d" % j], 16)
            rk[j], rv[j] = (S["cpk%d" % j], 16), (S["cpv%d" % j], 16)
        elif how[j][0] == "whole":
            rk[j] = rv[j] = (S["arrkv%d" % j], how[j][2])
        elif how[j][0] == "parts":
            rk[j], rv[j] = (S["arrk%d" % j], how[j][2]), (S["arrv%d" % j], how[j][2])

    vq.memset(T.zer[:, :], 0.0).then_inc(S.fill, 1)

    def mask_diag():
        g.wait_ge(S.fill, 1)
        g.affine_select(T.sel[:, :], T.zer[:, :], [[-1, 128]], AluOpType.is_equal, -200.0, 0, 1).then_inc(S.msk, 1)

    if not is_root:
        mask_diag()
    sent = send_all()
    if is_root:
        mask_diag()
    aq.wait_ge(S.msk, 1)
    aq.activation(T.ident[:, :], T.sel[:, :], Exp).then_inc(S.idn, 1)

    order = sorted(how, key=lambda b: how[b][1])
    E = [j for j in order if how[j][1] < 1] or order[:1]
    L = [j for j in order if j not in E]
    nE, nL = len(E), len(L)
    tardy = how[E[0]][1] >= 4
    stL = [T.stL0, T.stL1]
    trL = [T.trL0, T.trL1]
    O = [T.stE[:, 0:128], T.stL0[:, 0:128]]

    def early_pv():
        tq.wait_ge(S.cpe, 1)
        for j in E:
            tq.wait_ge(*rv[j])
        for h in H:
            for e, j in enumerate(E):
                c = (h * nE + e) * 128
                mm = tq.matmul(half(T.oE, h), T.ptE[:, c:c + 128], vv(j), e == 0, e == nE - 1)
                if e == nE - 1:
                    mm.then_inc(S.oe, 1)

    tq.wait_ge(S.ldq, 16)
    for e, j in enumerate(E):
        tq.wait_ge(*rk[j])
        for h in H:
            c = h * 256 + e * 128
            tq.matmul(T.stE[:, c:c + 128], half(T.qs, h), kk(j), True, True).then_inc(S.ste, 1)
    tq.wait_ge(S.idn, 1)
    tq.wait_ge(S.pxe, 2)
    for h in H:
        for e in range(nE):
            c = (h * nE + e) * 128
            tq.transpose(T.trE[:, c:c + 128], T.pE[:, h * 256 + e * 128:h * 256 + (e + 1) * 128],
                         T.ident[:, :]).then_inc(S.tre, 1)
    if not tardy:
        early_pv()
    tq.wait_ge(S.me, 2)
    if all(how[j][1] >= 6 for j in L):
        turns = [(l, h) for h in H for l in range(nL)]
    else:
        turns = [(l, h) for l in range(nL) for h in H]
    for l, h in turns:
        tq.wait_ge(*rk[L[l]])
        tq.matmul(stL[h][:, l * 128:(l + 1) * 128], half(T.qs, h), kk(L[l]), True, True).then_inc(S["stl%d" % h], 1)
    if tardy:
        early_pv()
    for h in H:
        for l in range(nL):
            tq.wait_ge(S["px%d%d" % (h, l)], 1)
            tq.transpose(trL[h][:, l * 128:(l + 1) * 128], T.pL[:, h * 256 + l * 128:h * 256 + (l + 1) * 128],
                         T.ident[:, :]).then_inc(S["trl%d" % h], 1)
    tq.wait_ge(S.ne, 2)
    tq.wait_ge(S.nl0, 1)
    for j in L:
        tq.wait_ge(*rv[j])
    for h in H:
        tq.wait_ge(S["cpl%d" % h], 1)
        for l, j in enumerate(L):
            mm = tq.matmul(O[h], T.ptL[:, h * 256 + l * 128:h * 256 + (l + 1) * 128], vv(j), l == 0, l == nL - 1)
            if l == nL - 1:
                mm.then_inc(S["o%d" % h], 1)

    vq.wait_ge(S.ste, 2 * nE)
    for h in H:
        vq.tensor_reduce(col(T.nm, h), T.stE[:, h * 256:h * 256 + nE * 128], X, amax, negate=True).then_inc(S.ne, 1)
    vq.wait_ge(S.ne, 2)
    for h in H:
        vq.tensor_scalar(col(stL[h], nL * 128), col(T.nm, h), -1.0, None, mult).then_inc(S.me, 1)
    vq.wait_ge(S.tre, 2 * nE)
    vq.tensor_copy(T.ptE[:, 0:2 * nE * 128], T.trE[:, 0:2 * nE * 128]).then_inc(S.cpe, 1)
    vq.wait_ge(S.me, 2)
    for h in H:
        vq.wait_ge(S["stl%d" % h], nL)
        vq.tensor_reduce(col(T.nm, 2 + h), stL[h][:, 0:nL * 128 + 1], X, amax, negate=True).then_inc(S["nl%d" % h], 1)
    for h in H:
        for l in range(nL):
            vq.wait_ge(S["px%d%d" % (h, l)], 1)
        vq.tensor_reduce(col(T.ls, h), T.lL[:, 2 * h:2 * h + nL], X, add).then_inc(S["ls%d" % h], 1)
        vq.wait_ge(S["trl%d" % h], nL)
        vq.tensor_copy(T.ptL[:, h * 256:h * 256 + nL * 128], trL[h][:, 0:nL * 128]).then_inc(S["cpl%d" % h], 1)
    vq.wait_ge(S.las, 2)
    vq.reciprocal(T.rl[:, 0:2], T.la[:, 0:2]).then_inc(S.rs, 1)
    vq.wait_ge(S.te, 2)
    for h in H:
        vq.wait_ge(S["o%d" % h], 1)
        vq.tensor_tensor(half(T.u, h), O[h], half(T.tE, h), add).then_inc(S["u%d" % h], 1)

    aq.wait_ge(S.ne, 2)
    for h in H:
        aq.activation(T.pE[:, h * 256:h * 256 + nE * 128], T.stE[:, h * 256:h * 256 + nE * 128], Exp,
                      bias=col(T.nm, h), accum_out=col(T.lE, h)).then_inc(S.pxe, 1)
    for h in H:
        aq.wait_ge(S["nl%d" % h], 1)
        for l in range(nL):
            aq.activation(T.pL[:, h * 256 + l * 128:h * 256 + (l + 1) * 128], stL[h][:, l * 128:(l + 1) * 128], Exp,
                          bias=col(T.nm, 2 + h), accum_out=col(T.lL, 2 * h + l)).then_inc(S["px%d%d" % (h, l)], 1)
    for h in H:
        aq.activation(col(T.w, h), col(T.nm, h), Exp, bias=col(T.nm, 2 + h), scale=-1.0).then_inc(S.w, 1)
    aq.wait_ge(S.w, 2)
    aq.wait_ge(S.pxe, 2)
    for h in H:
        aq.wait_ge(S["ls%d" % h], 1)
        aq.activation(col(T.la, h), col(T.lE, h), Ident, bias=col(T.ls, h), scale=col(T.w, h)).then_inc(S.las, 1)
    aq.wait_ge(S.oe, 2)
    for h in H:
        aq.activation(half(T.tE, h), half(T.oE, h), Ident, scale=col(T.w, h)).then_inc(S.te, 1)
    aq.wait_ge(S.rs, 1)
    for h in H:
        aq.wait_ge(S["u%d" % h], 1)
        aq.activation(half(T.ys, h), half(T.u, h), Ident, scale=col(T.rl, h)).then_inc(S["y%d" % h], 1)
    aq.wait_ge(S.y1, 1)
    aq.dma_start(T.y[128:256, :], half(T.ys, 1)).then_inc(S.st, 16)

    sq.wait_ge(S.y0, 1)
    sq.dma_start(T.y[0:128, :], half(T.ys, 0)).then_inc(S.st, 16)

    if sent:
        g.wait_ge(S.sent, sent)
    g.wait_ge(S.st, 32)
